import numpy as np
import ml_dtypes


def mxq(x, axis, fmt="e4m3"):
    dtype, down = {"e4m3": (ml_dtypes.float8_e4m3fn, 7), "e5m2": (ml_dtypes.float8_e5m2, 14)}[fmt]
    v = np.moveaxis(np.asarray(x, np.float32).astype(ml_dtypes.bfloat16).astype(np.float64), axis, -1)
    blocks = v.reshape(v.shape[:-1] + (-1, 32))
    amax = np.abs(blocks).max(-1, keepdims=True)
    byte = np.maximum(np.where(amax > 0, np.frexp(amax)[1] - 1 + 127, 0) - down, 1)
    scale = np.exp2(byte - 127.0)
    codes = (blocks / scale).astype(np.float32).astype(dtype).astype(np.float64)
    return np.moveaxis((codes * scale).reshape(v.shape), -1, axis)


WIDE = False


def mx_kscale(k):
    if not WIDE:
        return np.ones(k)
    levels = np.array([30, -30])
    if k % 512:
        return np.exp2(np.random.permutation(np.resize(levels, k // 32))).repeat(32)
    a = np.empty((k // 512, 16))
    for p in range(k // 512):
        a[p, :8] = np.random.permutation(np.resize(levels, 8))
        for g in range(8):
            far = levels[np.abs(levels - a[p, g]) >= 10]
            a[p, g + 8] = far[np.random.randint(len(far))]
    return np.exp2(a.ravel()).repeat(32)


def f64(x):
    return np.asarray(x).astype(np.float64)


def striped(idx):
    return np.tile(np.asarray(idx).reshape(-1, 16).T, (8, 1)).astype(np.uint16)


def unstriped(offs):
    return offs[:16].T.reshape(-1).astype(np.int64)


def striped8(idx):
    return np.asarray(idx).reshape(8, -1, 16).transpose(0, 2, 1).reshape(128, -1).astype(np.uint16)


def unstriped8(offs):
    return offs.reshape(8, 16, -1).transpose(0, 2, 1).reshape(8, -1).astype(np.int64)


def pick8(x, idx, run):
    r = np.arange(len(x))
    return x[r[:, None], idx[r % (8 * run) // run]]


E2M1 = np.array([0.0, 0.5, 1.0, 1.5, 2.0, 3.0, 4.0, 6.0, -0.0, -0.5, -1.0, -1.5, -2.0, -3.0, -4.0, -6.0])


def pack_weight(w, fmt):
    k, n = w.shape
    w = f64(np.asarray(w, np.float32).astype(ml_dtypes.bfloat16)).reshape(k // 32, 32, n)
    amax = np.abs(w).max(1)
    if fmt in ("e4m3", "e5m2"):
        byte = np.frexp(amax)[1] - 1 + 127 - (7 if fmt == "e4m3" else 14)
    else:
        mant, ex = np.frexp(amax / 6.0)
        byte = np.where(mant > 0.5, ex, ex - 1) + 127
    byte = np.clip(np.where(amax > 0, byte, 1), 1, 254)
    scaled = (w * np.exp2(127.0 - byte)[:, None, :]).reshape(k, n).astype(np.float32)
    by_word = np.ascontiguousarray(scaled.reshape(k // 512, 128, 4, n).transpose(0, 1, 3, 2))
    if fmt in ("e4m3", "e5m2"):
        words = by_word.astype(ml_dtypes.float8_e4m3fn if fmt == "e4m3" else ml_dtypes.float8_e5m2).view(np.uint8)
    else:
        c = by_word.astype(ml_dtypes.float4_e2m1fn).view(np.uint8) & 0xF
        words = (c[..., 0::2] | (c[..., 1::2] << 4)).reshape(k // 512, 128, 2 * n)
    return np.ascontiguousarray(words), np.ascontiguousarray(byte.astype(np.uint8).reshape(k // 512, 16, n))


def unpack_weight(words, scales, fmt):
    g, _, n = scales.shape
    words = np.ascontiguousarray(words).reshape(g, 128, n, -1)
    if fmt in ("e4m3", "e5m2"):
        vals = words.view(ml_dtypes.float8_e4m3fn if fmt == "e4m3" else ml_dtypes.float8_e5m2).astype(np.float64)
    else:
        nib = np.empty((g, 128, n, 4), np.uint8)
        nib[..., 0::2] = words & 0xF
        nib[..., 1::2] = words >> 4
        vals = E2M1[nib]
    vals = vals * np.repeat(np.exp2(scales.astype(np.float64) - 127.0), 8, axis=1)[..., None]
    return vals.transpose(0, 1, 3, 2).reshape(g * 512, n)


def sigmoid(v):
    return 1.0 / (1.0 + np.exp(-v))


def sgn(shape):
    return np.random.uniform(0.5, 2.0, shape) * np.where(np.random.standard_normal(shape) < 0, -1.0, 1.0)


K, T, J, R, F, Z, N, O = 512, 1024, 256, 512, 512, 1024, 256, 128


def setup_inputs():
    n = np.random.standard_normal
    idx = np.random.permutation(T)[:J]
    idx2 = np.random.permutation(Z)[:J]
    idx3 = np.stack([np.random.permutation(J)[:O] for _ in range(8)])
    idx4 = np.stack([np.random.permutation(J)[:O] for _ in range(8)])
    idx5 = np.random.permutation(J)[:O]
    fk = mx_kscale(K)
    ff = mx_kscale(F)
    fr = mx_kscale(R)
    xtp = pack_weight(n((K, T)) / fk[:, None], "e2m1")
    xop = pack_weight(n((F, Z)) / ff[:, None], "e4m3")
    wp = pack_weight(n((K, R)) * 1 / np.sqrt(K) * fk[:, None] * fr, "e4m3")
    w2p = pack_weight(n((K, R)) * 1 / np.sqrt(K) * fk[:, None] * fr, "e5m2")
    w0p = pack_weight(n((F, R)) * 1 / np.sqrt(F) * ff[:, None] * fr, "e5m2")
    wbp = pack_weight(n((R, N)) * 1 / np.sqrt(R) / fr[:, None], "e2m1")
    wcp = pack_weight(n((R, N)) * 1 / np.sqrt(R) / fr[:, None], "e5m2")
    return {
        "xt_words": xtp[0],
        "xt_scales": xtp[1],
        "xo_words": xop[0],
        "xo_scales": xop[1],
        "w_words": wp[0],
        "w_scales": wp[1],
        "w2_words": w2p[0],
        "w2_scales": w2p[1],
        "w0_words": w0p[0],
        "w0_scales": w0p[1],
        "wb_words": wbp[0],
        "wb_scales": wbp[1],
        "wc_words": wcp[0],
        "wc_scales": wcp[1],
        "so": (np.random.uniform(0.5, 1.6, (N, 1))).astype(np.float32),
        "sp": (sgn((N, 1))).astype(np.float32),
        "bo": (np.random.uniform(-2.0, 2.0, (N, 1))).astype(np.float32),
        "offs": striped(idx),
        "offs2": striped(idx2),
        "offs3": striped8(idx3),
        "offs4": striped8(idx4),
        "offs5": striped(idx5),
    }


def reference(xt_words, xt_scales, xo_words, xo_scales, w_words, w_scales, w2_words, w2_scales, w0_words, w0_scales, wb_words, wb_scales, wc_words, wc_scales, so, sp, bo, offs, offs2, offs3, offs4, offs5):
    idx = unstriped(offs)
    idx2 = unstriped(offs2)
    idx3 = unstriped8(offs3)
    idx4 = unstriped8(offs4)
    idx5 = unstriped(offs5)
    xtu = unpack_weight(xt_words, xt_scales, "e2m1")
    xou = unpack_weight(xo_words, xo_scales, "e4m3")
    wu = unpack_weight(w_words, w_scales, "e4m3")
    w2u = unpack_weight(w2_words, w2_scales, "e5m2")
    w0u = unpack_weight(w0_words, w0_scales, "e5m2")
    wbu = unpack_weight(wb_words, wb_scales, "e2m1")
    wcu = unpack_weight(wc_words, wc_scales, "e5m2")
    xtidxg = xtu[:, idx]
    a = wu.T @ xtidxg
    xoidx2g = xou[:, idx2]
    b = w2u.T @ xtidxg + w0u.T @ xoidx2g
    hid = np.abs(a - b)
    hidq = mxq(hid, 0, "e5m2")
    p = wbu.T @ hidq
    q = wcu.T @ hidq
    y = pick8(p, idx3, 16) * f64(so) * sigmoid(pick8(p, idx4, 16) * f64(sp) + f64(bo)) - q[:, idx5]
    return y

@@ -1,0 +1,222 @@
+from contextlib import ExitStack
+
+import concourse.mybir as mybir
+from concourse.masks import make_identity
+
+K, T, J, R, F, Z, N, O = 512, 1024, 256, 512, 512, 1024, 256, 128
+FLOPS = 2 * (2 * K * R * J + F * R * J + 2 * R * N * J)
+
+F32 = mybir.dt.float32
+BF16 = mybir.dt.bfloat16
+I32 = mybir.dt.int32
+U32 = mybir.dt.uint32
+U16 = mybir.dt.uint16
+U8 = mybir.dt.uint8
+E4M3 = mybir.dt.float8_e4m3fn_x4
+E5M2 = mybir.dt.float8_e5m2_x4
+E2M1 = mybir.dt.float4_e2m1fn_x4
+ACT = mybir.ActivationFunctionType
+ALU = mybir.AluOpType
+
+P = 128
+HALF = 64
+QUAD = 32
+PACK = 4
+TILES = 2
+
+
+def load_scale_rows(queue, stage, base, scales, col0, which=(0, 1)):
+    words = scales.shape[2] // 4
+    rows = scales[0].bitcast(I32).rearrange("(h q r) c -> q r h c", h=2, q=2)
+    for q in which:
+        first = base + QUAD * q
+        queue.dma_start(out=stage[first : first + PACK, :, col0 : col0 + words], in_=rows[q])
+
+
+def tile_list_outcomegatedgroups_leaned_kernel(
+    tc, xt_words, xt_scales, xo_words, xo_scales, w_words, w_scales, w2_words, w2_scales,
+    w0_words, w0_scales, wb_words, wb_scales, wc_words, wc_scales, so, sp, bo,
+    offs, offs2, offs3, offs4, offs5, out,
+):
+    nc = tc.nc
+    low, high = slice(0, HALF), slice(HALF, P)
+
+    with ExitStack() as ctx:
+        lists = ctx.enter_context(tc.tile_pool(name="lists", bufs=1))
+        keep = ctx.enter_context(tc.tile_pool(name="keep", bufs=1))
+        psum = ctx.enter_context(tc.psum_pool(name="psum", bufs=1))
+
+        tok_list = lists.tile([P, J // 16], U16, name="tok_list")
+        note_list = lists.tile([P, J // 16], U16, name="note_list")
+        value_list = lists.tile([P, O // 16], U16, name="value_list")
+        gate_list = lists.tile([P, O // 16], U16, name="gate_list")
+        second_list = lists.tile([P, O // 16], U16, name="second_list")
+
+        xt_stage = keep.tile([P, 2, T // 4], I32, name="xt_stage")
+        xo_stage = keep.tile([P, 2, Z // 4], I32, name="xo_stage")
+        w_rows = keep.tile([P, 2, R // 4], I32, name="w_rows", align_bytes=64)
+        w2_rows = keep.tile([P, 2, R // 4], I32, name="w2_rows", align_bytes=64)
+        w0_plane = keep.tile([P, 2, R // 4], I32, name="w0_plane", align_bytes=64)
+        out_planes = keep.tile([P, 2, 2 * N // 4], I32, name="out_planes", align_bytes=64)
+        ident = keep.tile([P, P], F32, name="ident")
+        nc.vector.memset(xt_stage[low], 0)
+        nc.vector.memset(w_rows[low], 0)
+        nc.vector.memset(w2_rows[low], 0)
+        nc.vector.memset(xo_stage[high], 0)
+        nc.vector.memset(w0_plane[high], 0)
+        nc.vector.memset(out_planes[high], 0)
+        nc.vector.memset(ident[:], 0.0)
+        make_identity(nc, ident[:], nomemset=True)
+
+        xt_codes = keep.tile([P, T], U16, name="xt_codes")
+        xo_codes = keep.tile([P, Z], U32, name="xo_codes")
+        w_codes = keep.tile([P, R], I32, name="w_codes", align_bytes=64)
+        w2_codes = keep.tile([P, R], I32, name="w2_codes", align_bytes=64)
+        w0_codes = keep.tile([P, R], I32, name="w0_codes", align_bytes=64)
+        wb_codes = keep.tile([P, 2 * N], U8, name="wb_codes", align_bytes=64)
+        wc_codes = keep.tile([P, N], I32, name="wc_codes", align_bytes=64)
+        so_cols = keep.tile([P, TILES], F32, name="so_cols")
+        sp_cols = keep.tile([P, TILES], F32, name="sp_cols")
+        bo_cols = keep.tile([P, TILES], F32, name="bo_cols")
+
+        def words_of(x_words):
+            return x_words[0].rearrange("p c t -> p (c t)").bitcast(I32)
+
+        nc.sync.dma_start(tok_list[:], offs)
+        nc.sync.dma_start(xt_codes[:].bitcast(I32), xt_words[0].bitcast(I32))
+        load_scale_rows(nc.sync, xt_stage, 0, xt_scales, 0)
+        load_scale_rows(nc.sync, w_rows, 0, w_scales, 0)
+        nc.sync.dma_start(w_codes[:], words_of(w_words))
+        nc.sync.dma_start(xo_codes[:].bitcast(I32), words_of(xo_words))
+        load_scale_rows(nc.sync, w2_rows, 0, w2_scales, 0)
+        load_scale_rows(nc.sync, xo_stage, HALF, xo_scales, 0)
+        nc.sync.dma_start(note_list[:], offs2)
+        nc.sync.dma_start(w2_codes[:], words_of(w2_words))
+        nc.sync.dma_start(w0_codes[:], words_of(w0_words))
+        load_scale_rows(nc.sync, w0_plane, HALF, w0_scales, 0)
+        nc.sync.dma_start(wb_codes[:].bitcast(I32), wb_words[0].bitcast(I32))
+        nc.sync.dma_start(wc_codes[:], words_of(wc_words))
+        load_scale_rows(nc.sync, out_planes, HALF, wb_scales, 0)
+        load_scale_rows(nc.sync, out_planes, HALF, wc_scales, N // 4)
+        nc.sync.dma_start(gate_list[:], offs4)
+        nc.sync.dma_start(value_list[:], offs3)
+        nc.sync.dma_start(second_list[:], offs5)
+        with nc.allow_non_contiguous_dma(reason="one value a partition for each tile of output features"):
+            for cols, vec in ((sp_cols, sp), (bo_cols, bo), (so_cols, so)):
+                nc.sync.dma_start(cols[:], vec.rearrange("(c p) o -> p (c o)", p=P))
+
+        xt_plane = keep.tile([P, T], U8, name="xt_plane")
+        xo_plane = keep.tile([P, Z], U8, name="xo_plane")
+        xt_codes_g = [keep.tile([P, P], U16, name=f"xt_codes_g{s}", align_bytes=64) for s in range(TILES)]
+        xt_plane_g = [keep.tile([P, P], U8, name=f"xt_plane_g{s}", align_bytes=64) for s in range(TILES)]
+        xo_codes_g = [keep.tile([P, P], U32, name=f"xo_codes_g{s}", align_bytes=64) for s in range(TILES)]
+        xo_plane_g = [keep.tile([P, P], U8, name=f"xo_plane_g{s}", align_bytes=64) for s in range(TILES)]
+
+        def gather(codes_g, plane_g, codes, plane, slot_list):
+            for s in range(TILES):
+                entries = slot_list[:, s * (P // 16) : (s + 1) * (P // 16)]
+                nc.vector.tensor_copy(plane_g[s][:], plane[:].indirect(entries))
+                nc.vector.tensor_copy(codes_g[s][:], codes[:].indirect(entries))
+
+        nc.vector.tensor_copy(xt_plane[low].bitcast(I32), xt_stage[low, 0, :])
+        nc.vector.tensor_copy(xt_plane[high].bitcast(I32), xt_stage[low, 1, :])
+        nc.vector.tensor_copy(w_rows[high, 0, :], w_rows[low, 1, :])
+        gather(xt_codes_g, xt_plane_g, xt_codes, xt_plane, tok_list)
+        nc.vector.tensor_copy(w2_rows[high, 0, :], w2_rows[low, 1, :])
+        nc.vector.tensor_copy(xo_plane[high].bitcast(I32), xo_stage[high, 1, :])
+        nc.vector.tensor_copy(xo_plane[low].bitcast(I32), xo_stage[high, 0, :])
+        nc.vector.tensor_copy(w0_plane[low, 1, :], w0_plane[high, 0, :])
+        gather(xo_codes_g, xo_plane_g, xo_codes, xo_plane, note_list)
+        nc.vector.tensor_copy(out_planes[low, 1, :], out_planes[high, 0, :])
+
+        w_plane = w_rows[:, 0, :].bitcast(U8)
+        w2_plane = w2_rows[:, 0, :].bitcast(U8)
+        wb_plane = out_planes[:, 1, 0 : N // 4].bitcast(U8)
+        wc_plane = out_planes[:, 1, N // 4 :].bitcast(U8)
+
+        a_ps = [psum.tile([P, R], F32, name=f"a_ps{s}", tag=f"first{s}") for s in range(TILES)]
+        b_ps = [psum.tile([P, R], F32, name=f"b_ps{s}") for s in range(TILES)]
+        for s in range(TILES):
+            nc.tensor.matmul_mx(
+                out=a_ps[s][:], lhsT=xt_codes_g[s][:].bitcast(E2M1), lhsT_scale=xt_plane_g[s][:],
+                rhs=w_codes[:].bitcast(E4M3), rhs_scale=w_plane, start=True, stop=True,
+            )
+        for s in range(TILES):
+            nc.tensor.matmul_mx(
+                out=b_ps[s][:], lhsT=xt_codes_g[s][:].bitcast(E2M1), lhsT_scale=xt_plane_g[s][:],
+                rhs=w2_codes[:].bitcast(E5M2), rhs_scale=w2_plane, start=True, stop=False,
+            )
+        for s in range(TILES):
+            nc.tensor.matmul_mx(
+                out=b_ps[s][:], lhsT=xo_codes_g[s][:].bitcast(E4M3), lhsT_scale=xo_plane_g[s][:],
+                rhs=w0_codes[:].bitcast(E5M2), rhs_scale=w0_plane[:, 1, :].bitcast(U8), start=False, stop=True,
+            )
+
+        a_sb = [keep.tile([P, PACK, P], F32, name=f"a_sb{s}") for s in range(TILES)]
+        diff = [keep.tile([P, PACK, P], F32, name=f"diff{s}") for s in range(TILES)]
+        turned = [psum.tile([P, PACK, P], F32, name=f"turned{s}") for s in range(TILES)]
+        hid = [keep.tile([P, P, PACK], BF16, name=f"hid{s}", align_bytes=64) for s in range(TILES)]
+        hid_codes = [keep.tile([P, P], U32, name=f"hid_codes{s}", align_bytes=64) for s in range(TILES)]
+        hid_plane = [keep.tile([P, P], U8, name=f"hid_plane{s}", align_bytes=64) for s in range(TILES)]
+        for s in range(TILES):
+            nc.scalar.copy(a_sb[s][:], a_ps[s][:].rearrange("j (p t) -> j t p", t=PACK))
+        for s in range(TILES):
+            nc.vector.tensor_tensor(
+                diff[s][:], a_sb[s][:], b_ps[s][:].rearrange("j (p t) -> j t p", t=PACK), ALU.subtract
+            )
+        for s in range(TILES):
+            for t in range(PACK):
+                nc.tensor.transpose(turned[s][:, t, :], diff[s][:, t, :], ident[:])
+        for s in range(TILES):
+            nc.scalar.activation(hid[s][:], turned[s][:].rearrange("p t j -> p j t"), ACT.Abs)
+
+        early = psum.tile([P, 2 * TILES, P], F32, name="early", tag="first0")
+        late_p = [psum.tile([P, P], F32, name=f"late_p{c}") for c in range(TILES)]
+        late_q = psum.tile([P, TILES, P], F32, name="late_q", tag="first1")
+        p_ps = [[early[:, c, :], late_p[c][:]] for c in range(TILES)]
+        q_ps = [[early[:, TILES + c, :], late_q[:, c, :]] for c in range(TILES)]
+        for s in range(TILES):
+            nc.vector.quantize_mx(
+                out=hid_codes[s][:].bitcast(E5M2), scales=hid_plane[s][:],
+                in_=hid[s][:].rearrange("p j t -> p (j t)"),
+            )
+            for c in range(TILES):
+                nc.tensor.matmul_mx(
+                    out=p_ps[c][s], lhsT=wb_codes[:, 2 * P * c : 2 * P * (c + 1)].bitcast(E2M1),
+                    lhsT_scale=wb_plane[:, P * c : P * (c + 1)],
+                    rhs=hid_codes[s][:].bitcast(E5M2), rhs_scale=hid_plane[s][:], start=True, stop=True,
+                )
+            for c in range(TILES):
+                nc.tensor.matmul_mx(
+                    out=q_ps[c][s], lhsT=wc_codes[:, P * c : P * (c + 1)].bitcast(E5M2),
+                    lhsT_scale=wc_plane[:, P * c : P * (c + 1)],
+                    rhs=hid_codes[s][:].bitcast(E5M2), rhs_scale=hid_plane[s][:], start=True, stop=True,
+                )
+
+        p_sb = [keep.tile([P, J], F32, name=f"p_sb{c}") for c in range(TILES)]
+        q_sb = keep.tile([P, TILES, J], F32, name="q_sb")
+        for c in range(TILES):
+            nc.scalar.copy(p_sb[c][:, 0:P], p_ps[c][0])
+        nc.vector.tensor_copy(q_sb[:, :, 0:P], early[:, TILES:, :])
+        nc.scalar.copy(p_sb[0][:, P:], p_ps[0][1])
+        nc.vector.tensor_copy(p_sb[1][:, P:], p_ps[1][1])
+        nc.vector.tensor_copy(q_sb[:, :, P:], late_q[:])
+
+        gate = [keep.tile([P, O], F32, name=f"gate{c}") for c in range(TILES)]
+        value = [keep.tile([P, O], F32, name=f"value{c}") for c in range(TILES)]
+        second = [keep.tile([P, O], F32, name=f"second{c}") for c in range(TILES)]
+        gated = [keep.tile([P, O], F32, name=f"gated{c}") for c in range(TILES)]
+        result = [keep.tile([P, O], F32, name=f"result{c}") for c in range(TILES)]
+        for c in range(TILES):
+            nc.vector.tensor_copy(second[c][:], q_sb[:, c, :].indirect(second_list[:]))
+        for c in range(TILES):
+            nc.scalar.activation(
+                gate[c][:], p_sb[c][:].indirect(gate_list[:]), ACT.Sigmoid,
+                bias=bo_cols[:, c : c + 1], scale=sp_cols[:, c : c + 1],
+            )
+            nc.scalar.activation(
+                value[c][:], p_sb[c][:].indirect(value_list[:]), ACT.Copy, scale=so_cols[:, c : c + 1]
+            )
+            nc.vector.tensor_tensor(gated[c][:], value[c][:], gate[c][:], ALU.mult)
+            nc.vector.tensor_tensor(result[c][:], gated[c][:], second[c][:], ALU.subtract)
+            nc.sync.dma_start(out[P * c : P * (c + 1), :], result[c][:])

@@ -23,6 +23,7 @@ HALF = 64
 QUAD = 32
 PACK = 4
 TILES = 2
+QUADS = 4
 
 
 def load_scale_rows(queue, stage, base, scales, col0, which=(0, 1)):
@@ -55,18 +56,20 @@ def tile_list_outcomegatedgroups_leaned_kernel(
         xt_stage = keep.tile([P, 2, T // 4], I32, name="xt_stage")
         xo_stage = keep.tile([P, 2, Z // 4], I32, name="xo_stage")
         w_rows = keep.tile([P, 2, R // 4], I32, name="w_rows", align_bytes=64)
-        w2_rows = keep.tile([P, 2, R // 4], I32, name="w2_rows", align_bytes=64)
-        w0_plane = keep.tile([P, 2, R // 4], I32, name="w0_plane", align_bytes=64)
+        b_rows = keep.tile([P, QUADS, 2 * R // 4], I32, name="b_rows", align_bytes=64)
         out_planes = keep.tile([P, 2, 2 * N // 4], I32, name="out_planes", align_bytes=64)
         ident = keep.tile([P, P], F32, name="ident")
-        nc.vector.memset(xt_stage[low], 0)
         nc.vector.memset(w_rows[low], 0)
-        nc.vector.memset(w2_rows[low], 0)
-        nc.vector.memset(xo_stage[high], 0)
-        nc.vector.memset(w0_plane[high], 0)
+        nc.vector.memset(xt_stage[high], 0)
+        nc.vector.memset(b_rows[:, 0, :], 0)
+        nc.vector.memset(xo_stage[low], 0)
         nc.vector.memset(out_planes[high], 0)
         nc.vector.memset(ident[:], 0.0)
         make_identity(nc, ident[:], nomemset=True)
+
+        warm = keep.tile([P, 2], F32, name="warm")
+        nc.gpsimd.memset(warm[:, 0:1], 0.0)
+        nc.scalar.activation(warm[:, 1:2], warm[:, 0:1], ACT.Sigmoid)
 
         xt_codes = keep.tile([P, T], U16, name="xt_codes")
         xo_codes = keep.tile([P, Z], U32, name="xo_codes")
@@ -84,20 +87,20 @@ def tile_list_outcomegatedgroups_leaned_kernel(
 
         nc.sync.dma_start(tok_list[:], offs)
         nc.sync.dma_start(xt_codes[:].bitcast(I32), xt_words[0].bitcast(I32))
-        load_scale_rows(nc.sync, xt_stage, 0, xt_scales, 0)
         load_scale_rows(nc.sync, w_rows, 0, w_scales, 0)
+        load_scale_rows(nc.sync, xt_stage, HALF, xt_scales, 0)
         nc.sync.dma_start(w_codes[:], words_of(w_words))
+        nc.sync.dma_start(b_rows[0:PACK, :, 0 : R // 4], w2_scales[0].bitcast(I32).rearrange("(q r) c -> r q c", r=PACK))
         nc.sync.dma_start(xo_codes[:].bitcast(I32), words_of(xo_words))
-        load_scale_rows(nc.sync, w2_rows, 0, w2_scales, 0)
-        load_scale_rows(nc.sync, xo_stage, HALF, xo_scales, 0)
+        nc.sync.dma_start(b_rows[0:PACK, :, R // 4 :], w0_scales[0].bitcast(I32).rearrange("(q r) c -> r q c", r=PACK))
+        load_scale_rows(nc.sync, xo_stage, 0, xo_scales, 0)
         nc.sync.dma_start(note_list[:], offs2)
         nc.sync.dma_start(w2_codes[:], words_of(w2_words))
         nc.sync.dma_start(w0_codes[:], words_of(w0_words))
-        load_scale_rows(nc.sync, w0_plane, HALF, w0_scales, 0)
-        nc.sync.dma_start(wb_codes[:].bitcast(I32), wb_words[0].bitcast(I32))
-        nc.sync.dma_start(wc_codes[:], words_of(wc_words))
         load_scale_rows(nc.sync, out_planes, HALF, wb_scales, 0)
         load_scale_rows(nc.sync, out_planes, HALF, wc_scales, N // 4)
+        nc.sync.dma_start(wb_codes[:].bitcast(I32), wb_words[0].bitcast(I32))
+        nc.sync.dma_start(wc_codes[:], words_of(wc_words))
         nc.sync.dma_start(gate_list[:], offs4)
         nc.sync.dma_start(value_list[:], offs3)
         nc.sync.dma_start(second_list[:], offs5)
@@ -118,19 +121,20 @@ def tile_list_outcomegatedgroups_leaned_kernel(
                 nc.vector.tensor_copy(plane_g[s][:], plane[:].indirect(entries))
                 nc.vector.tensor_copy(codes_g[s][:], codes[:].indirect(entries))
 
-        nc.vector.tensor_copy(xt_plane[low].bitcast(I32), xt_stage[low, 0, :])
-        nc.vector.tensor_copy(xt_plane[high].bitcast(I32), xt_stage[low, 1, :])
         nc.vector.tensor_copy(w_rows[high, 0, :], w_rows[low, 1, :])
+        nc.vector.tensor_copy(xt_plane[high].bitcast(I32), xt_stage[high, 1, :])
+        nc.vector.tensor_copy(xt_plane[low].bitcast(I32), xt_stage[high, 0, :])
         gather(xt_codes_g, xt_plane_g, xt_codes, xt_plane, tok_list)
-        nc.vector.tensor_copy(w2_rows[high, 0, :], w2_rows[low, 1, :])
-        nc.vector.tensor_copy(xo_plane[high].bitcast(I32), xo_stage[high, 1, :])
-        nc.vector.tensor_copy(xo_plane[low].bitcast(I32), xo_stage[high, 0, :])
-        nc.vector.tensor_copy(w0_plane[low, 1, :], w0_plane[high, 0, :])
+        for q in range(1, QUADS):
+            nc.vector.tensor_copy(b_rows[QUAD * q : QUAD * q + PACK, 0, :], b_rows[0:PACK, q, :])
+        nc.vector.tensor_copy(xo_plane[low].bitcast(I32), xo_stage[low, 0, :])
+        nc.vector.tensor_copy(xo_plane[high].bitcast(I32), xo_stage[low, 1, :])
         gather(xo_codes_g, xo_plane_g, xo_codes, xo_plane, note_list)
         nc.vector.tensor_copy(out_planes[low, 1, :], out_planes[high, 0, :])
 
         w_plane = w_rows[:, 0, :].bitcast(U8)
-        w2_plane = w2_rows[:, 0, :].bitcast(U8)
+        w2_plane = b_rows[:, 0, 0 : R // 4].bitcast(U8)
+        w0_plane = b_rows[:, 0, R // 4 :].bitcast(U8)
         wb_plane = out_planes[:, 1, 0 : N // 4].bitcast(U8)
         wc_plane = out_planes[:, 1, N // 4 :].bitcast(U8)
 
@@ -149,58 +153,57 @@ def tile_list_outcomegatedgroups_leaned_kernel(
         for s in range(TILES):
             nc.tensor.matmul_mx(
                 out=b_ps[s][:], lhsT=xo_codes_g[s][:].bitcast(E4M3), lhsT_scale=xo_plane_g[s][:],
-                rhs=w0_codes[:].bitcast(E5M2), rhs_scale=w0_plane[:, 1, :].bitcast(U8), start=False, stop=True,
+                rhs=w0_codes[:].bitcast(E5M2), rhs_scale=w0_plane, start=False, stop=True,
             )
 
         a_sb = [keep.tile([P, PACK, P], F32, name=f"a_sb{s}") for s in range(TILES)]
         diff = [keep.tile([P, PACK, P], F32, name=f"diff{s}") for s in range(TILES)]
         turned = [psum.tile([P, PACK, P], F32, name=f"turned{s}") for s in range(TILES)]
         hid = [keep.tile([P, P, PACK], BF16, name=f"hid{s}", align_bytes=64) for s in range(TILES)]
-        hid_codes = [keep.tile([P, P], U32, name=f"hid_codes{s}", align_bytes=64) for s in range(TILES)]
-        hid_plane = [keep.tile([P, P], U8, name=f"hid_plane{s}", align_bytes=64) for s in range(TILES)]
+        hid_codes = keep.tile([P, J], U32, name="hid_codes", align_bytes=64)
+        hid_plane = keep.tile([P, J], U8, name="hid_plane", align_bytes=64)
         for s in range(TILES):
             nc.scalar.copy(a_sb[s][:], a_ps[s][:].rearrange("j (p t) -> j t p", t=PACK))
         for s in range(TILES):
-            nc.vector.tensor_tensor(
-                diff[s][:], a_sb[s][:], b_ps[s][:].rearrange("j (p t) -> j t p", t=PACK), ALU.subtract
-            )
+            b_by_slot = b_ps[s][:].rearrange("j (p t) -> j t p", t=PACK)
+            for pair in (slice(0, 2), slice(2, 4)):
+                nc.vector.tensor_tensor(diff[s][:, pair, :], a_sb[s][:, pair, :], b_by_slot[:, pair, :], ALU.subtract)
         for s in range(TILES):
             for t in range(PACK):
                 nc.tensor.transpose(turned[s][:, t, :], diff[s][:, t, :], ident[:])
         for s in range(TILES):
             nc.scalar.activation(hid[s][:], turned[s][:].rearrange("p t j -> p j t"), ACT.Abs)
 
-        early = psum.tile([P, 2 * TILES, P], F32, name="early", tag="first0")
+        early_p = psum.tile([P, TILES, P], F32, name="early_p", tag="first0")
         late_p = [psum.tile([P, P], F32, name=f"late_p{c}") for c in range(TILES)]
-        late_q = psum.tile([P, TILES, P], F32, name="late_q", tag="first1")
-        p_ps = [[early[:, c, :], late_p[c][:]] for c in range(TILES)]
-        q_ps = [[early[:, TILES + c, :], late_q[:, c, :]] for c in range(TILES)]
+        q_ps = psum.tile([P, TILES, J], F32, name="q_ps", tag="first1")
+        p_ps = [[early_p[:, c, :], late_p[c][:]] for c in range(TILES)]
         for s in range(TILES):
+            slots = slice(P * s, P * (s + 1))
             nc.vector.quantize_mx(
-                out=hid_codes[s][:].bitcast(E5M2), scales=hid_plane[s][:],
+                out=hid_codes[:, slots].bitcast(E5M2), scales=hid_plane[:, slots],
                 in_=hid[s][:].rearrange("p j t -> p (j t)"),
             )
             for c in range(TILES):
                 nc.tensor.matmul_mx(
                     out=p_ps[c][s], lhsT=wb_codes[:, 2 * P * c : 2 * P * (c + 1)].bitcast(E2M1),
                     lhsT_scale=wb_plane[:, P * c : P * (c + 1)],
-                    rhs=hid_codes[s][:].bitcast(E5M2), rhs_scale=hid_plane[s][:], start=True, stop=True,
+                    rhs=hid_codes[:, slots].bitcast(E5M2), rhs_scale=hid_plane[:, slots], start=True, stop=True,
                 )
-            for c in range(TILES):
-                nc.tensor.matmul_mx(
-                    out=q_ps[c][s], lhsT=wc_codes[:, P * c : P * (c + 1)].bitcast(E5M2),
-                    lhsT_scale=wc_plane[:, P * c : P * (c + 1)],
-                    rhs=hid_codes[s][:].bitcast(E5M2), rhs_scale=hid_plane[s][:], start=True, stop=True,
-                )
+        for c in range(TILES):
+            nc.tensor.matmul_mx(
+                out=q_ps[:, c, :], lhsT=wc_codes[:, P * c : P * (c + 1)].bitcast(E5M2),
+                lhsT_scale=wc_plane[:, P * c : P * (c + 1)],
+                rhs=hid_codes[:].bitcast(E5M2), rhs_scale=hid_plane[:], start=True, stop=True,
+            )
 
         p_sb = [keep.tile([P, J], F32, name=f"p_sb{c}") for c in range(TILES)]
         q_sb = keep.tile([P, TILES, J], F32, name="q_sb")
         for c in range(TILES):
             nc.scalar.copy(p_sb[c][:, 0:P], p_ps[c][0])
-        nc.vector.tensor_copy(q_sb[:, :, 0:P], early[:, TILES:, :])
         nc.scalar.copy(p_sb[0][:, P:], p_ps[0][1])
         nc.vector.tensor_copy(p_sb[1][:, P:], p_ps[1][1])
-        nc.vector.tensor_copy(q_sb[:, :, P:], late_q[:])
+        nc.vector.tensor_copy(q_sb[:], q_ps[:])
 
         gate = [keep.tile([P, O], F32, name=f"gate{c}") for c in range(TILES)]
         value = [keep.tile([P, O], F32, name=f"value{c}") for c in range(TILES)]

@@ -62,8 +62,8 @@ def tile_list_outcomegatedgroups_leaned_kernel(
         nc.vector.memset(w_rows[low], 0)
         nc.vector.memset(xt_stage[high], 0)
         nc.vector.memset(b_rows[:, 0, :], 0)
-        nc.vector.memset(xo_stage[low], 0)
-        nc.vector.memset(out_planes[high], 0)
+        nc.vector.memset(xo_stage[high], 0)
+        nc.vector.memset(out_planes[low], 0)
         nc.vector.memset(ident[:], 0.0)
         make_identity(nc, ident[:], nomemset=True)
 
@@ -87,18 +87,20 @@ def tile_list_outcomegatedgroups_leaned_kernel(
 
         nc.sync.dma_start(tok_list[:], offs)
         nc.sync.dma_start(xt_codes[:].bitcast(I32), xt_words[0].bitcast(I32))
-        load_scale_rows(nc.sync, w_rows, 0, w_scales, 0)
-        load_scale_rows(nc.sync, xt_stage, HALF, xt_scales, 0)
+        for q in range(2):
+            load_scale_rows(nc.sync, w_rows, 0, w_scales, 0, (q,))
+            load_scale_rows(nc.sync, xt_stage, HALF, xt_scales, 0, (q,))
         nc.sync.dma_start(w_codes[:], words_of(w_words))
         nc.sync.dma_start(b_rows[0:PACK, :, 0 : R // 4], w2_scales[0].bitcast(I32).rearrange("(q r) c -> r q c", r=PACK))
         nc.sync.dma_start(xo_codes[:].bitcast(I32), words_of(xo_words))
+        load_scale_rows(nc.sync, xo_stage, HALF, xo_scales, 0, (0,))
         nc.sync.dma_start(b_rows[0:PACK, :, R // 4 :], w0_scales[0].bitcast(I32).rearrange("(q r) c -> r q c", r=PACK))
-        load_scale_rows(nc.sync, xo_stage, 0, xo_scales, 0)
+        load_scale_rows(nc.sync, xo_stage, HALF, xo_scales, 0, (1,))
         nc.sync.dma_start(note_list[:], offs2)
         nc.sync.dma_start(w2_codes[:], words_of(w2_words))
         nc.sync.dma_start(w0_codes[:], words_of(w0_words))
-        load_scale_rows(nc.sync, out_planes, HALF, wb_scales, 0)
-        load_scale_rows(nc.sync, out_planes, HALF, wc_scales, N // 4)
+        load_scale_rows(nc.sync, out_planes, 0, wb_scales, 0)
+        load_scale_rows(nc.sync, out_planes, 0, wc_scales, N // 4)
         nc.sync.dma_start(wb_codes[:].bitcast(I32), wb_words[0].bitcast(I32))
         nc.sync.dma_start(wc_codes[:], words_of(wc_words))
         nc.sync.dma_start(gate_list[:], offs4)
@@ -127,16 +129,16 @@ def tile_list_outcomegatedgroups_leaned_kernel(
         gather(xt_codes_g, xt_plane_g, xt_codes, xt_plane, tok_list)
         for q in range(1, QUADS):
             nc.vector.tensor_copy(b_rows[QUAD * q : QUAD * q + PACK, 0, :], b_rows[0:PACK, q, :])
-        nc.vector.tensor_copy(xo_plane[low].bitcast(I32), xo_stage[low, 0, :])
-        nc.vector.tensor_copy(xo_plane[high].bitcast(I32), xo_stage[low, 1, :])
+        nc.vector.tensor_copy(xo_plane[high].bitcast(I32), xo_stage[high, 1, :])
+        nc.vector.tensor_copy(xo_plane[low].bitcast(I32), xo_stage[high, 0, :])
         gather(xo_codes_g, xo_plane_g, xo_codes, xo_plane, note_list)
-        nc.vector.tensor_copy(out_planes[low, 1, :], out_planes[high, 0, :])
+        nc.vector.tensor_copy(out_planes[high, 0, :], out_planes[low, 1, :])
 
         w_plane = w_rows[:, 0, :].bitcast(U8)
         w2_plane = b_rows[:, 0, 0 : R // 4].bitcast(U8)
         w0_plane = b_rows[:, 0, R // 4 :].bitcast(U8)
-        wb_plane = out_planes[:, 1, 0 : N // 4].bitcast(U8)
-        wc_plane = out_planes[:, 1, N // 4 :].bitcast(U8)
+        wb_plane = out_planes[:, 0, 0 : N // 4].bitcast(U8)
+        wc_plane = out_planes[:, 0, N // 4 :].bitcast(U8)
 
         a_ps = [psum.tile([P, R], F32, name=f"a_ps{s}", tag=f"first{s}") for s in range(TILES)]
         b_ps = [psum.tile([P, R], F32, name=f"b_ps{s}") for s in range(TILES)]
@@ -162,12 +164,20 @@ def tile_list_outcomegatedgroups_leaned_kernel(
         hid = [keep.tile([P, P, PACK], BF16, name=f"hid{s}", align_bytes=64) for s in range(TILES)]
         hid_codes = keep.tile([P, J], U32, name="hid_codes", align_bytes=64)
         hid_plane = keep.tile([P, J], U8, name="hid_plane", align_bytes=64)
+        def from_psum(bank):
+            return bank[:].rearrange("j (g i t) -> j g t i", i=PACK, t=PACK)
+
+        def by_slot(tile):
+            return tile[:].rearrange("j t (g i) -> j g t i", i=PACK)
+
         for s in range(TILES):
-            nc.scalar.copy(a_sb[s][:], a_ps[s][:].rearrange("j (p t) -> j t p", t=PACK))
+            nc.scalar.copy(by_slot(a_sb[s]), from_psum(a_ps[s]))
         for s in range(TILES):
-            b_by_slot = b_ps[s][:].rearrange("j (p t) -> j t p", t=PACK)
             for pair in (slice(0, 2), slice(2, 4)):
-                nc.vector.tensor_tensor(diff[s][:, pair, :], a_sb[s][:, pair, :], b_by_slot[:, pair, :], ALU.subtract)
+                nc.vector.tensor_tensor(
+                    by_slot(diff[s])[:, :, pair, :], by_slot(a_sb[s])[:, :, pair, :],
+                    from_psum(b_ps[s])[:, :, pair, :], ALU.subtract,
+                )
         for s in range(TILES):
             for t in range(PACK):
                 nc.tensor.transpose(turned[s][:, t, :], diff[s][:, t, :], ident[:])

from contextlib import ExitStack

import concourse.mybir as mybir
from concourse.masks import make_identity

K, T, J, R, F, Z, N, O = 512, 1024, 256, 512, 512, 1024, 256, 128
FLOPS = 2 * (2 * K * R * J + F * R * J + 2 * R * N * J)

F32 = mybir.dt.float32
BF16 = mybir.dt.bfloat16
I32 = mybir.dt.int32
U32 = mybir.dt.uint32
U16 = mybir.dt.uint16
U8 = mybir.dt.uint8
E4M3 = mybir.dt.float8_e4m3fn_x4
E5M2 = mybir.dt.float8_e5m2_x4
E2M1 = mybir.dt.float4_e2m1fn_x4
ACT = mybir.ActivationFunctionType
ALU = mybir.AluOpType

P = 128
HALF = 64
QUAD = 32
PACK = 4
TILES = 2
QUADS = 4


def load_scale_rows(queue, stage, base, scales, col0, which=(0, 1)):
    words = scales.shape[2] // 4
    rows = scales[0].bitcast(I32).rearrange("(h q r) c -> q r h c", h=2, q=2)
    for q in which:
        first = base + QUAD * q
        queue.dma_start(out=stage[first : first + PACK, :, col0 : col0 + words], in_=rows[q])


def tile_list_outcomegatedgroups_leaned_kernel(
    tc, xt_words, xt_scales, xo_words, xo_scales, w_words, w_scales, w2_words, w2_scales,
    w0_words, w0_scales, wb_words, wb_scales, wc_words, wc_scales, so, sp, bo,
    offs, offs2, offs3, offs4, offs5, out,
):
    nc = tc.nc
    low, high = slice(0, HALF), slice(HALF, P)

    with ExitStack() as ctx:
        lists = ctx.enter_context(tc.tile_pool(name="lists", bufs=1))
        keep = ctx.enter_context(tc.tile_pool(name="keep", bufs=1))
        psum = ctx.enter_context(tc.psum_pool(name="psum", bufs=1))

        tok_list = lists.tile([P, J // 16], U16, name="tok_list")
        note_list = lists.tile([P, J // 16], U16, name="note_list")
        value_list = lists.tile([P, O // 16], U16, name="value_list")
        gate_list = lists.tile([P, O // 16], U16, name="gate_list")
        second_list = lists.tile([P, O // 16], U16, name="second_list")

        xt_stage = keep.tile([P, 2, T // 4], I32, name="xt_stage")
        xo_stage = keep.tile([P, 2, Z // 4], I32, name="xo_stage")
        w_rows = keep.tile([P, 2, R // 4], I32, name="w_rows", align_bytes=64)
        b_rows = keep.tile([P, QUADS, 2 * R // 4], I32, name="b_rows", align_bytes=64)
        out_planes = keep.tile([P, 2, 2 * N // 4], I32, name="out_planes", align_bytes=64)
        ident = keep.tile([P, P], F32, name="ident")
        nc.vector.memset(w_rows[low], 0)
        nc.vector.memset(xt_stage[high], 0)
        nc.vector.memset(b_rows[:, 0, :], 0)
        nc.vector.memset(xo_stage[high], 0)
        nc.vector.memset(out_planes[low], 0)
        nc.vector.memset(ident[:], 0.0)
        make_identity(nc, ident[:], nomemset=True)

        warm = keep.tile([P, 2], F32, name="warm")
        nc.gpsimd.memset(warm[:, 0:1], 0.0)
        nc.scalar.activation(warm[:, 1:2], warm[:, 0:1], ACT.Sigmoid)

        xt_codes = keep.tile([P, T], U16, name="xt_codes")
        xo_codes = keep.tile([P, Z], U32, name="xo_codes")
        w_codes = keep.tile([P, R], I32, name="w_codes", align_bytes=64)
        w2_codes = keep.tile([P, R], I32, name="w2_codes", align_bytes=64)
        w0_codes = keep.tile([P, R], I32, name="w0_codes", align_bytes=64)
        wb_codes = keep.tile([P, 2 * N], U8, name="wb_codes", align_bytes=64)
        wc_codes = keep.tile([P, N], I32, name="wc_codes", align_bytes=64)
        so_cols = keep.tile([P, TILES], F32, name="so_cols")
        sp_cols = keep.tile([P, TILES], F32, name="sp_cols")
        bo_cols = keep.tile([P, TILES], F32, name="bo_cols")

        def words_of(x_words):
            return x_words[0].rearrange("p c t -> p (c t)").bitcast(I32)

        nc.sync.dma_start(tok_list[:], offs)
        nc.sync.dma_start(xt_codes[:].bitcast(I32), xt_words[0].bitcast(I32))
        for q in range(2):
            load_scale_rows(nc.sync, w_rows, 0, w_scales, 0, (q,))
            load_scale_rows(nc.sync, xt_stage, HALF, xt_scales, 0, (q,))
        nc.sync.dma_start(w_codes[:], words_of(w_words))
        nc.sync.dma_start(b_rows[0:PACK, :, 0 : R // 4], w2_scales[0].bitcast(I32).rearrange("(q r) c -> r q c", r=PACK))
        nc.sync.dma_start(xo_codes[:].bitcast(I32), words_of(xo_words))
        load_scale_rows(nc.sync, xo_stage, HALF, xo_scales, 0, (0,))
        nc.sync.dma_start(b_rows[0:PACK, :, R // 4 :], w0_scales[0].bitcast(I32).rearrange("(q r) c -> r q c", r=PACK))
        load_scale_rows(nc.sync, xo_stage, HALF, xo_scales, 0, (1,))
        nc.sync.dma_start(note_list[:], offs2)
        nc.sync.dma_start(w2_codes[:], words_of(w2_words))
        nc.sync.dma_start(w0_codes[:], words_of(w0_words))
        load_scale_rows(nc.sync, out_planes, 0, wb_scales, 0)
        load_scale_rows(nc.sync, out_planes, 0, wc_scales, N // 4)
        nc.sync.dma_start(wb_codes[:].bitcast(I32), wb_words[0].bitcast(I32))
        nc.sync.dma_start(wc_codes[:], words_of(wc_words))
        nc.sync.dma_start(gate_list[:], offs4)
        nc.sync.dma_start(value_list[:], offs3)
        nc.sync.dma_start(second_list[:], offs5)
        with nc.allow_non_contiguous_dma(reason="one value a partition for each tile of output features"):
            for cols, vec in ((sp_cols, sp), (bo_cols, bo), (so_cols, so)):
                nc.sync.dma_start(cols[:], vec.rearrange("(c p) o -> p (c o)", p=P))

        xt_plane = keep.tile([P, T], U8, name="xt_plane")
        xo_plane = keep.tile([P, Z], U8, name="xo_plane")
        xt_codes_g = [keep.tile([P, P], U16, name=f"xt_codes_g{s}", align_bytes=64) for s in range(TILES)]
        xt_plane_g = [keep.tile([P, P], U8, name=f"xt_plane_g{s}", align_bytes=64) for s in range(TILES)]
        xo_codes_g = [keep.tile([P, P], U32, name=f"xo_codes_g{s}", align_bytes=64) for s in range(TILES)]
        xo_plane_g = [keep.tile([P, P], U8, name=f"xo_plane_g{s}", align_bytes=64) for s in range(TILES)]

        def gather(codes_g, plane_g, codes, plane, slot_list):
            for s in range(TILES):
                entries = slot_list[:, s * (P // 16) : (s + 1) * (P // 16)]
                nc.vector.tensor_copy(plane_g[s][:], plane[:].indirect(entries))
                nc.vector.tensor_copy(codes_g[s][:], codes[:].indirect(entries))

        nc.vector.tensor_copy(w_rows[high, 0, :], w_rows[low, 1, :])
        nc.vector.tensor_copy(xt_plane[high].bitcast(I32), xt_stage[high, 1, :])
        nc.vector.tensor_copy(xt_plane[low].bitcast(I32), xt_stage[high, 0, :])
        gather(xt_codes_g, xt_plane_g, xt_codes, xt_plane, tok_list)
        for q in range(1, QUADS):
            nc.vector.tensor_copy(b_rows[QUAD * q : QUAD * q + PACK, 0, :], b_rows[0:PACK, q, :])
        nc.vector.tensor_copy(xo_plane[high].bitcast(I32), xo_stage[high, 1, :])
        nc.vector.tensor_copy(xo_plane[low].bitcast(I32), xo_stage[high, 0, :])
        gather(xo_codes_g, xo_plane_g, xo_codes, xo_plane, note_list)
        nc.vector.tensor_copy(out_planes[high, 0, :], out_planes[low, 1, :])

        w_plane = w_rows[:, 0, :].bitcast(U8)
        w2_plane = b_rows[:, 0, 0 : R // 4].bitcast(U8)
        w0_plane = b_rows[:, 0, R // 4 :].bitcast(U8)
        wb_plane = out_planes[:, 0, 0 : N // 4].bitcast(U8)
        wc_plane = out_planes[:, 0, N // 4 :].bitcast(U8)

        a_ps = [psum.tile([P, R], F32, name=f"a_ps{s}", tag=f"first{s}") for s in range(TILES)]
        b_ps = [psum.tile([P, R], F32, name=f"b_ps{s}") for s in range(TILES)]
        for s in range(TILES):
            nc.tensor.matmul_mx(
                out=a_ps[s][:], lhsT=xt_codes_g[s][:].bitcast(E2M1), lhsT_scale=xt_plane_g[s][:],
                rhs=w_codes[:].bitcast(E4M3), rhs_scale=w_plane, start=True, stop=True,
            )
        for s in range(TILES):
            nc.tensor.matmul_mx(
                out=b_ps[s][:], lhsT=xt_codes_g[s][:].bitcast(E2M1), lhsT_scale=xt_plane_g[s][:],
                rhs=w2_codes[:].bitcast(E5M2), rhs_scale=w2_plane, start=True, stop=False,
            )
        for s in range(TILES):
            nc.tensor.matmul_mx(
                out=b_ps[s][:], lhsT=xo_codes_g[s][:].bitcast(E4M3), lhsT_scale=xo_plane_g[s][:],
                rhs=w0_codes[:].bitcast(E5M2), rhs_scale=w0_plane, start=False, stop=True,
            )

        a_sb = [keep.tile([P, PACK, P], F32, name=f"a_sb{s}") for s in range(TILES)]
        diff = [keep.tile([P, PACK, P], F32, name=f"diff{s}") for s in range(TILES)]
        turned = [psum.tile([P, PACK, P], F32, name=f"turned{s}") for s in range(TILES)]
        hid = [keep.tile([P, P, PACK], BF16, name=f"hid{s}", align_bytes=64) for s in range(TILES)]
        hid_codes = keep.tile([P, J], U32, name="hid_codes", align_bytes=64)
        hid_plane = keep.tile([P, J], U8, name="hid_plane", align_bytes=64)
        def from_psum(bank):
            return bank[:].rearrange("j (g i t) -> j g t i", i=PACK, t=PACK)

        def by_slot(tile):
            return tile[:].rearrange("j t (g i) -> j g t i", i=PACK)

        for s in range(TILES):
            nc.scalar.copy(by_slot(a_sb[s]), from_psum(a_ps[s]))
        for s in range(TILES):
            for pair in (slice(0, 2), slice(2, 4)):
                nc.vector.tensor_tensor(
                    by_slot(diff[s])[:, :, pair, :], by_slot(a_sb[s])[:, :, pair, :],
                    from_psum(b_ps[s])[:, :, pair, :], ALU.subtract,
                )
        for s in range(TILES):
            for t in range(PACK):
                nc.tensor.transpose(turned[s][:, t, :], diff[s][:, t, :], ident[:])
        for s in range(TILES):
            nc.scalar.activation(hid[s][:], turned[s][:].rearrange("p t j -> p j t"), ACT.Abs)

        early_p = psum.tile([P, TILES, P], F32, name="early_p", tag="first0")
        late_p = [psum.tile([P, P], F32, name=f"late_p{c}") for c in range(TILES)]
        q_ps = psum.tile([P, TILES, J], F32, name="q_ps", tag="first1")
        p_ps = [[early_p[:, c, :], late_p[c][:]] for c in range(TILES)]
        for s in range(TILES):
            slots = slice(P * s, P * (s + 1))
            nc.vector.quantize_mx(
                out=hid_codes[:, slots].bitcast(E5M2), scales=hid_plane[:, slots],
                in_=hid[s][:].rearrange("p j t -> p (j t)"),
            )
            for c in range(TILES):
                nc.tensor.matmul_mx(
                    out=p_ps[c][s], lhsT=wb_codes[:, 2 * P * c : 2 * P * (c + 1)].bitcast(E2M1),
                    lhsT_scale=wb_plane[:, P * c : P * (c + 1)],
                    rhs=hid_codes[:, slots].bitcast(E5M2), rhs_scale=hid_plane[:, slots], start=True, stop=True,
                )
        for c in range(TILES):
            nc.tensor.matmul_mx(
                out=q_ps[:, c, :], lhsT=wc_codes[:, P * c : P * (c + 1)].bitcast(E5M2),
                lhsT_scale=wc_plane[:, P * c : P * (c + 1)],
                rhs=hid_codes[:].bitcast(E5M2), rhs_scale=hid_plane[:], start=True, stop=True,
            )

        p_sb = [keep.tile([P, J], F32, name=f"p_sb{c}") for c in range(TILES)]
        q_sb = keep.tile([P, TILES, J], F32, name="q_sb")
        for c in range(TILES):
            nc.scalar.copy(p_sb[c][:, 0:P], p_ps[c][0])
        nc.scalar.copy(p_sb[0][:, P:], p_ps[0][1])
        nc.vector.tensor_copy(p_sb[1][:, P:], p_ps[1][1])
        nc.vector.tensor_copy(q_sb[:], q_ps[:])

        gate = [keep.tile([P, O], F32, name=f"gate{c}") for c in range(TILES)]
        value = [keep.tile([P, O], F32, name=f"value{c}") for c in range(TILES)]
        second = [keep.tile([P, O], F32, name=f"second{c}") for c in range(TILES)]
        gated = [keep.tile([P, O], F32, name=f"gated{c}") for c in range(TILES)]
        result = [keep.tile([P, O], F32, name=f"result{c}") for c in range(TILES)]
        for c in range(TILES):
            nc.vector.tensor_copy(second[c][:], q_sb[:, c, :].indirect(second_list[:]))
        for c in range(TILES):
            nc.scalar.activation(
                gate[c][:], p_sb[c][:].indirect(gate_list[:]), ACT.Sigmoid,
                bias=bo_cols[:, c : c + 1], scale=sp_cols[:, c : c + 1],
            )
            nc.scalar.activation(
                value[c][:], p_sb[c][:].indirect(value_list[:]), ACT.Copy, scale=so_cols[:, c : c + 1]
            )
            nc.vector.tensor_tensor(gated[c][:], value[c][:], gate[c][:], ALU.mult)
            nc.vector.tensor_tensor(result[c][:], gated[c][:], second[c][:], ALU.subtract)
            nc.sync.dma_start(out[P * c : P * (c + 1), :], result[c][:])
